import numpy as np
import ml_dtypes


def mxq(x, axis, fmt="e4m3"):
    dtype, down = {"e4m3": (ml_dtypes.float8_e4m3fn, 7), "e5m2": (ml_dtypes.float8_e5m2, 14)}[fmt]
    v = np.moveaxis(np.asarray(x, np.float32).astype(ml_dtypes.bfloat16).astype(np.float64), axis, -1)
    blocks = v.reshape(v.shape[:-1] + (-1, 32))
    amax = np.abs(blocks).max(-1, keepdims=True)
    byte = np.maximum(np.where(amax > 0, np.frexp(amax)[1] - 1 + 127, 0) - down, 1)
    scale = np.exp2(byte - 127.0)
    codes = (blocks / scale).astype(np.float32).astype(dtype).astype(np.float64)
    return np.moveaxis((codes * scale).reshape(v.shape), -1, axis)


WIDE = False


def mx_kscale(k):
    if not WIDE:
        return np.ones(k)
    levels = np.array([10, -10, 5, -5, 0])
    if k % 512:
        return np.exp2(np.random.permutation(np.resize(levels, k // 32))).repeat(32)
    a = np.empty((k // 512, 16))
    for p in range(k // 512):
        a[p, :8] = np.random.permutation(np.resize(levels, 8))
        for g in range(8):
            far = levels[np.abs(levels - a[p, g]) >= 10]
            a[p, g + 8] = far[np.random.randint(len(far))]
    return np.exp2(a.ravel()).repeat(32)


def f64(x):
    return np.asarray(x).astype(np.float64)


def striped(idx):
    return np.tile(np.asarray(idx).reshape(-1, 16).T, (8, 1)).astype(np.uint16)


def unstriped(offs):
    return offs[:16].T.reshape(-1).astype(np.int64)


E2M1 = np.array([0.0, 0.5, 1.0, 1.5, 2.0, 3.0, 4.0, 6.0, -0.0, -0.5, -1.0, -1.5, -2.0, -3.0, -4.0, -6.0])


def pack_weight(w, fmt):
    k, n = w.shape
    w = f64(np.asarray(w, np.float32).astype(ml_dtypes.bfloat16)).reshape(k // 32, 32, n)
    amax = np.abs(w).max(1)
    if fmt == "e4m3":
        byte = np.frexp(amax)[1] - 1 + 127 - 7
    else:
        mant, ex = np.frexp(amax / 6.0)
        byte = np.where(mant > 0.5, ex, ex - 1) + 127
    byte = np.clip(np.where(amax > 0, byte, 1), 1, 254)
    scaled = (w * np.exp2(127.0 - byte)[:, None, :]).reshape(k, n).astype(np.float32)
    by_word = np.ascontiguousarray(scaled.reshape(k // 512, 128, 4, n).transpose(0, 1, 3, 2))
    if fmt == "e4m3":
        words = by_word.astype(ml_dtypes.float8_e4m3fn).view(np.uint8)
    else:
        c = by_word.astype(ml_dtypes.float4_e2m1fn).view(np.uint8) & 0xF
        words = (c[..., 0::2] | (c[..., 1::2] << 4)).reshape(k // 512, 128, 2 * n)
    return np.ascontiguousarray(words), np.ascontiguousarray(byte.astype(np.uint8).reshape(k // 512, 16, n))


def unpack_weight(words, scales, fmt):
    g, _, n = scales.shape
    words = np.ascontiguousarray(words).reshape(g, 128, n, -1)
    if fmt == "e4m3":
        vals = words.view(ml_dtypes.float8_e4m3fn).astype(np.float64)
    else:
        nib = np.empty((g, 128, n, 4), np.uint8)
        nib[..., 0::2] = words & 0xF
        nib[..., 1::2] = words >> 4
        vals = E2M1[nib]
    vals = vals * np.repeat(np.exp2(scales.astype(np.float64) - 127.0), 8, axis=1)[..., None]
    return vals.transpose(0, 1, 3, 2).reshape(g * 512, n)


def bf(x):
    return np.asarray(x, np.float32).astype(ml_dtypes.bfloat16)


def planes(Y):
    r, m = Y.shape
    b = f64(bf(Y)).reshape(r // 32, 32, m)
    amax = np.abs(b).max(1)
    byte = np.clip(np.where(amax > 0, np.frexp(amax)[1] - 1 + 127 - 7, 1), 1, 254)
    codes = (b * np.exp2(127.0 - byte)[:, None, :]).reshape(r, m).astype(np.float32).astype(ml_dtypes.float8_e4m3fn).view(np.uint8)
    words = codes.reshape(r // 512, 128, 4, m).transpose(0, 1, 3, 2)
    return np.ascontiguousarray(words), np.ascontiguousarray(byte.astype(np.uint8).reshape(r // 512, 16, m))


K, T, J, R, V, N = 512, 2048, 512, 512, 1024, 512


def setup_inputs():
    n = np.random.standard_normal
    idx = np.random.permutation(T)[:J]
    idx2 = np.random.permutation(V)[:J]
    fk = mx_kscale(K)
    fr = mx_kscale(R)
    xtp = pack_weight(n((K, T)) / fk[:, None], "e2m1")
    wap = pack_weight(n((K, R)) * 1 / np.sqrt(K) * fk[:, None] * fr, "e4m3")
    wbp = pack_weight(n((R, N)) * 1 / np.sqrt(R) / fr[:, None], "e2m1")
    return {
        "xt_words": xtp[0],
        "xt_scales": xtp[1],
        "wa_words": wap[0],
        "wa_scales": wap[1],
        "tb": (n((R, V)) * fr[:, None]).astype(np.float32),
        "wb_words": wbp[0],
        "wb_scales": wbp[1],
        "offs": striped(idx),
        "offs2": striped(idx2),
    }


def reference(xt_words, xt_scales, wa_words, wa_scales, tb, wb_words, wb_scales, offs, offs2):
    idx = unstriped(offs)
    idx2 = unstriped(offs2)
    xtu = unpack_weight(xt_words, xt_scales, "e2m1")
    wau = unpack_weight(wa_words, wa_scales, "e4m3")
    wbu = unpack_weight(wb_words, wb_scales, "e2m1")
    xtidxg = xtu[:, idx]
    a = wau.T @ xtidxg
    hid = np.maximum(a, 0.0) + f64(tb)[:, idx2]
    hidq = mxq(hid, 0, "e4m3")
    y = wbu.T @ hidq
    words, scales = planes(y)
    return y, words, scales

@@ -1,0 +1,180 @@
+from contextlib import ExitStack
+
+import concourse.mybir as mybir
+from concourse.masks import make_identity
+
+K, T, J, R, V, N = 512, 2048, 512, 512, 1024, 512
+FLOPS = 2 * K * R * J + 2 * R * N * J
+
+F32 = mybir.dt.float32
+BF16 = mybir.dt.bfloat16
+I32 = mybir.dt.int32
+U32 = mybir.dt.uint32
+U16 = mybir.dt.uint16
+U8 = mybir.dt.uint8
+FP8X4 = mybir.dt.float8_e4m3fn_x4
+FP4X4 = mybir.dt.float4_e2m1fn_x4
+ADD = mybir.AluOpType.add
+RELU = mybir.ActivationFunctionType.Relu
+
+P = 128
+PACK = 4
+QUADS = 4
+CH = 128
+CHUNKS = J // CH
+
+
+def load_scale_rows(queue, plane, rows):
+    for q in range(QUADS):
+        queue.dma_start(
+            out=plane[32 * q : 32 * q + 4, :].bitcast(I32),
+            in_=rows[0, 4 * q : 4 * q + 4, :].bitcast(I32),
+        )
+
+
+def tile_list_hidden_plus_table_pl_kernel(
+    tc, xt_words, xt_scales, wa_words, wa_scales, tb, wb_words, wb_scales, offs, offs2, out_0, out_1, out_2
+):
+    nc = tc.nc
+    with ExitStack() as ctx:
+        sb = ctx.enter_context(tc.tile_pool(name="sb", bufs=1))
+        ps = ctx.enter_context(tc.psum_pool(name="ps", bufs=1))
+
+        tok = sb.tile([P, J // 16], U16, name="tok")
+        ent = sb.tile([P, J // 16], U16, name="ent")
+        xw = sb.tile([P, T], U16, name="xw", align_bytes=64)
+        xs = sb.tile([P, T], U8, name="xs", align_bytes=64)
+        wa = sb.tile([P, R], U32, name="wa", align_bytes=64)
+        was = sb.tile([P, R], U8, name="was", align_bytes=64)
+        wb = sb.tile([P, N], U16, name="wb", align_bytes=64)
+        wbs = sb.tile([P, N], U8, name="wbs", align_bytes=64)
+        tb01 = sb.tile([P, 2, V], F32, name="tb01", align_bytes=64)
+        tb23 = sb.tile([P, 2, V], F32, name="tb23", align_bytes=64)
+        tbt = [tb01[:, 0, :], tb01[:, 1, :], tb23[:, 0, :], tb23[:, 1, :]]
+        ident = sb.tile([P, P], F32, name="ident", align_bytes=64)
+
+        nc.vector.memset(xs[:].bitcast(I32), 0)
+        nc.gpsimd.memset(wbs[:].bitcast(I32), 0)
+        make_identity(nc, ident[:])
+
+        tb_rows = tb.rearrange("(p t) v -> p t v", t=PACK)
+        nc.sync.dma_start(out=xw[:].bitcast(I32), in_=xt_words[0].bitcast(I32))
+        load_scale_rows(nc.sync, xs, xt_scales)
+        nc.sync.dma_start(tok[:], offs)
+        nc.sync.dma_start(ent[:], offs2)
+        nc.sync.dma_start(out=tb01[:], in_=tb_rows[:, 0:2, :])
+        load_scale_rows(nc.gpsimd, wbs, wb_scales)
+        nc.sync.dma_start(out=wa[:].bitcast(I32), in_=wa_words[0].rearrange("p n t -> p (n t)").bitcast(I32))
+        load_scale_rows(nc.sync, was, wa_scales)
+        nc.sync.dma_start(out=wb[:].bitcast(I32), in_=wb_words[0].bitcast(I32))
+        nc.sync.dma_start(out=tb23[:], in_=tb_rows[:, 2:4, :])
+
+        wbd = sb.tile([P, N], U16, name="wbd", align_bytes=64)
+        wbsd = sb.tile([P, N], U8, name="wbsd", align_bytes=64)
+
+        xg = sb.tile([P, J], U16, name="xg", align_bytes=64)
+        xsg = sb.tile([P, J], U8, name="xsg", align_bytes=64)
+        nc.vector.tensor_copy(out=xg[:], in_=xw[:].indirect(tok[:]))
+        g = sb.tile([P, PACK, J], F32, name="g", align_bytes=64)
+        nc.vector.tensor_copy(out=xsg[:], in_=xs[:].indirect(tok[:]))
+        for t in range(2):
+            nc.vector.tensor_copy(out=g[:, t, :], in_=tbt[t].indirect(ent[:]))
+
+        relu_t = []
+        for c in range(CHUNKS):
+            cols = slice(c * CH, (c + 1) * CH)
+            a_t = ps.tile([P, R], F32, name="a_t%d" % c, tag="mm%d" % c)
+            nc.tensor.matmul_mx(
+                out=a_t[:], lhsT=xg[:, cols].bitcast(FP4X4), lhsT_scale=xsg[:, cols],
+                rhs=wa[:].bitcast(FP8X4), rhs_scale=was[:], start=True, stop=True,
+            )
+            ra = sb.tile([P, PACK, P], F32, name="ra%d" % c, align_bytes=64)
+            nc.scalar.activation(out=ra[:], in_=a_t[:].rearrange("j (m t) -> j t m", t=PACK), func=RELU)
+            relu_t.append(ra)
+        relu_ps = []
+        for c in range(CHUNKS):
+            rp = ps.tile([P, PACK, CH], F32, name="rp%d" % c)
+            for t in range(PACK):
+                nc.tensor.transpose(rp[:, t, :], relu_t[c][:, t, :], ident[:])
+            relu_ps.append(rp)
+
+        hq = sb.tile([P, J], U32, name="hq", align_bytes=64)
+        hs = sb.tile([P, J], U8, name="hs", align_bytes=64)
+        yq = sb.tile([P, J], U32, name="yq", align_bytes=64)
+        ys = sb.tile([P, J], U8, name="ys", align_bytes=64)
+        out_rows = out_0.rearrange("(p t) j -> p t j", t=PACK)
+        out_words = out_1[0].rearrange("p j t -> p (j t)").bitcast(I32)
+        hb = [sb.tile([P, CH * PACK], BF16, name="hb%d" % c, align_bytes=64) for c in range(CHUNKS)]
+        yb = [sb.tile([P, CH * PACK], BF16, name="yb%d" % c, align_bytes=64) for c in range(CHUNKS)]
+        yf = [sb.tile([P, PACK, CH], F32, name="yf%d" % c, align_bytes=64) for c in range(CHUNKS)]
+
+        def gather_half(t, h):
+            half = J // 2
+            nc.vector.tensor_copy(
+                out=g[:, t, h * half : (h + 1) * half],
+                in_=tbt[t].indirect(ent[:, h * half // 16 : (h + 1) * half // 16]),
+            )
+
+        def add_table(c):
+            cols = slice(c * CH, (c + 1) * CH)
+            nc.vector.tensor_tensor(
+                out=hb[c][:].rearrange("p (c i t) -> p c t i", i=4, t=PACK),
+                in0=relu_ps[c][:].rearrange("p t (c i) -> p c t i", i=4),
+                in1=g[:, :, cols].rearrange("p t (c i) -> p c t i", i=4),
+                op=ADD,
+            )
+
+        def second_product(c):
+            cols = slice(c * CH, (c + 1) * CH)
+            nc.vector.quantize_mx(out=hq[:, cols].bitcast(FP8X4), scales=hs[:, cols], in_=hb[c][:])
+            y = ps.tile([P, PACK, CH], F32, name="y%d" % c, tag="mm%d" % c)
+            for t in range(PACK):
+                w_cols = slice(t * P, (t + 1) * P)
+                nc.tensor.matmul_mx(
+                    out=y[:, t, :], lhsT=wbd[:, w_cols].bitcast(FP4X4), lhsT_scale=wbsd[:, w_cols],
+                    rhs=hq[:, cols].bitcast(FP8X4), rhs_scale=hs[:, cols], start=True, stop=True,
+                )
+            yb_view = yb[c][:].rearrange("p (j t) -> p j t", t=PACK)
+            y_view = y[:].rearrange("p t j -> p j t")
+            if c == CHUNKS - 1:
+                nc.vector.tensor_copy(out=yb_view, in_=y_view)
+            else:
+                nc.scalar.copy(out=yb_view, in_=y_view)
+            nc.scalar.copy(out=yf[c][:], in_=y[:])
+            nc.sync.dma_start(out=out_rows[:, :, cols], in_=yf[c][:])
+
+        def planes(c):
+            cols = slice(c * CH, (c + 1) * CH)
+            nc.vector.quantize_mx(out=yq[:, cols].bitcast(FP8X4), scales=ys[:, cols], in_=yb[c][:])
+
+        nc.vector.tensor_copy(
+            out=wbd[:].rearrange("p (t m) -> p t m", t=PACK), in_=wb[:].rearrange("p (m t) -> p t m", t=PACK)
+        )
+        gather_half(2, 0)
+        gather_half(3, 0)
+        nc.vector.tensor_copy(
+            out=wbsd[:].rearrange("p (t m) -> p t m", t=PACK), in_=wbs[:].rearrange("p (m t) -> p t m", t=PACK)
+        )
+        add_table(0)
+        gather_half(2, 1)
+        second_product(0)
+        add_table(1)
+        gather_half(3, 1)
+        second_product(1)
+        add_table(2)
+        planes(0)
+        second_product(2)
+        add_table(3)
+        planes(1)
+        second_product(3)
+        planes(2)
+        early = slice(0, J - CH)
+        nc.sync.dma_start(out=out_words[:, early], in_=yq[:, early].bitcast(I32))
+        planes(3)
+        late = slice(J - CH, J)
+        nc.sync.dma_start(out=out_words[:, late], in_=yq[:, late].bitcast(I32))
+        for q in range(QUADS):
+            queue = nc.sync if q % 2 == 0 else nc.scalar
+            queue.dma_start(
+                out=out_2[0, 4 * q : 4 * q + 4, :].bitcast(I32), in_=ys[32 * q : 32 * q + 4, :].bitcast(I32)
+            )

@@ -27,8 +27,8 @@ CHUNKS = J // CH
 def load_scale_rows(queue, plane, rows):
     for q in range(QUADS):
         queue.dma_start(
-            out=plane[32 * q : 32 * q + 4, :].bitcast(I32),
-            in_=rows[0, 4 * q : 4 * q + 4, :].bitcast(I32),
+            out=plane[q:P:32, :].bitcast(I32),
+            in_=rows[0, q:16:4, :].bitcast(I32),
         )
 
 
@@ -48,9 +48,7 @@ def tile_list_hidden_plus_table_pl_kernel(
         was = sb.tile([P, R], U8, name="was", align_bytes=64)
         wb = sb.tile([P, N], U16, name="wb", align_bytes=64)
         wbs = sb.tile([P, N], U8, name="wbs", align_bytes=64)
-        tb01 = sb.tile([P, 2, V], F32, name="tb01", align_bytes=64)
-        tb23 = sb.tile([P, 2, V], F32, name="tb23", align_bytes=64)
-        tbt = [tb01[:, 0, :], tb01[:, 1, :], tb23[:, 0, :], tb23[:, 1, :]]
+        tbt = [sb.tile([P, V], F32, name="tb%d" % t, align_bytes=64)[:] for t in range(PACK)]
         ident = sb.tile([P, P], F32, name="ident", align_bytes=64)
 
         nc.vector.memset(xs[:].bitcast(I32), 0)
@@ -58,26 +56,31 @@ def tile_list_hidden_plus_table_pl_kernel(
         make_identity(nc, ident[:])
 
         tb_rows = tb.rearrange("(p t) v -> p t v", t=PACK)
+        nc.sync.dma_start(tok[:], offs)
+        nc.sync.dma_start(out=wb[:].bitcast(I32), in_=wb_words[0].bitcast(I32))
         nc.sync.dma_start(out=xw[:].bitcast(I32), in_=xt_words[0].bitcast(I32))
         load_scale_rows(nc.sync, xs, xt_scales)
-        nc.sync.dma_start(tok[:], offs)
         nc.sync.dma_start(ent[:], offs2)
-        nc.sync.dma_start(out=tb01[:], in_=tb_rows[:, 0:2, :])
-        load_scale_rows(nc.gpsimd, wbs, wb_scales)
         nc.sync.dma_start(out=wa[:].bitcast(I32), in_=wa_words[0].rearrange("p n t -> p (n t)").bitcast(I32))
+        nc.sync.dma_start(out=tbt[0], in_=tb_rows[:, 0, :])
         load_scale_rows(nc.sync, was, wa_scales)
-        nc.sync.dma_start(out=wb[:].bitcast(I32), in_=wb_words[0].bitcast(I32))
-        nc.sync.dma_start(out=tb23[:], in_=tb_rows[:, 2:4, :])
+        for t in range(1, PACK - 1):
+            nc.sync.dma_start(out=tbt[t], in_=tb_rows[:, t, :])
+        load_scale_rows(nc.sync, wbs, wb_scales)
+        nc.sync.dma_start(out=tbt[PACK - 1], in_=tb_rows[:, PACK - 1, :])
 
         wbd = sb.tile([P, N], U16, name="wbd", align_bytes=64)
         wbsd = sb.tile([P, N], U8, name="wbsd", align_bytes=64)
 
+        nc.vector.tensor_copy(
+            out=wbd[:].rearrange("p (t m) -> p t m", t=PACK), in_=wb[:].rearrange("p (m t) -> p t m", t=PACK)
+        )
         xg = sb.tile([P, J], U16, name="xg", align_bytes=64)
         xsg = sb.tile([P, J], U8, name="xsg", align_bytes=64)
         nc.vector.tensor_copy(out=xg[:], in_=xw[:].indirect(tok[:]))
         g = sb.tile([P, PACK, J], F32, name="g", align_bytes=64)
         nc.vector.tensor_copy(out=xsg[:], in_=xs[:].indirect(tok[:]))
-        for t in range(2):
+        for t in range(PACK):
             nc.vector.tensor_copy(out=g[:, t, :], in_=tbt[t].indirect(ent[:]))
 
         relu_t = []
@@ -108,19 +111,12 @@ def tile_list_hidden_plus_table_pl_kernel(
         yb = [sb.tile([P, CH * PACK], BF16, name="yb%d" % c, align_bytes=64) for c in range(CHUNKS)]
         yf = [sb.tile([P, PACK, CH], F32, name="yf%d" % c, align_bytes=64) for c in range(CHUNKS)]
 
-        def gather_half(t, h):
-            half = J // 2
-            nc.vector.tensor_copy(
-                out=g[:, t, h * half : (h + 1) * half],
-                in_=tbt[t].indirect(ent[:, h * half // 16 : (h + 1) * half // 16]),
-            )
-
         def add_table(c):
             cols = slice(c * CH, (c + 1) * CH)
             nc.vector.tensor_tensor(
-                out=hb[c][:].rearrange("p (c i t) -> p c t i", i=4, t=PACK),
-                in0=relu_ps[c][:].rearrange("p t (c i) -> p c t i", i=4),
-                in1=g[:, :, cols].rearrange("p t (c i) -> p c t i", i=4),
+                out=hb[c][:].rearrange("p (c i t) -> p c t i", i=2, t=PACK),
+                in0=relu_ps[c][:].rearrange("p t (c i) -> p c t i", i=2),
+                in1=g[:, :, cols].rearrange("p t (c i) -> p c t i", i=2),
                 op=ADD,
             )
 
@@ -134,40 +130,31 @@ def tile_list_hidden_plus_table_pl_kernel(
                     out=y[:, t, :], lhsT=wbd[:, w_cols].bitcast(FP4X4), lhsT_scale=wbsd[:, w_cols],
                     rhs=hq[:, cols].bitcast(FP8X4), rhs_scale=hs[:, cols], start=True, stop=True,
                 )
-            yb_view = yb[c][:].rearrange("p (j t) -> p j t", t=PACK)
-            y_view = y[:].rearrange("p t j -> p j t")
-            if c == CHUNKS - 1:
-                nc.vector.tensor_copy(out=yb_view, in_=y_view)
-            else:
-                nc.scalar.copy(out=yb_view, in_=y_view)
             nc.scalar.copy(out=yf[c][:], in_=y[:])
             nc.sync.dma_start(out=out_rows[:, :, cols], in_=yf[c][:])
+
+        def round_stored(c):
+            nc.vector.tensor_copy(
+                out=yb[c][:].rearrange("p (c i t) -> p c t i", i=2, t=PACK),
+                in_=yf[c][:].rearrange("p t (c i) -> p c t i", i=2),
+            )
 
         def planes(c):
             cols = slice(c * CH, (c + 1) * CH)
             nc.vector.quantize_mx(out=yq[:, cols].bitcast(FP8X4), scales=ys[:, cols], in_=yb[c][:])
 
         nc.vector.tensor_copy(
-            out=wbd[:].rearrange("p (t m) -> p t m", t=PACK), in_=wb[:].rearrange("p (m t) -> p t m", t=PACK)
-        )
-        gather_half(2, 0)
-        gather_half(3, 0)
-        nc.vector.tensor_copy(
             out=wbsd[:].rearrange("p (t m) -> p t m", t=PACK), in_=wbs[:].rearrange("p (m t) -> p t m", t=PACK)
         )
         add_table(0)
-        gather_half(2, 1)
-        second_product(0)
-        add_table(1)
-        gather_half(3, 1)
-        second_product(1)
-        add_table(2)
-        planes(0)
-        second_product(2)
-        add_table(3)
-        planes(1)
-        second_product(3)
-        planes(2)
+        for c in range(1, CHUNKS):
+            add_table(c)
+            second_product(c - 1)
+        second_product(CHUNKS - 1)
+        round_stored(0)
+        for c in range(1, CHUNKS):
+            round_stored(c)
+            planes(c - 1)
         early = slice(0, J - CH)
         nc.sync.dma_start(out=out_words[:, early], in_=yq[:, early].bitcast(I32))
         planes(3)

@@ -57,31 +57,29 @@ def tile_list_hidden_plus_table_pl_kernel(
 
         tb_rows = tb.rearrange("(p t) v -> p t v", t=PACK)
         nc.sync.dma_start(tok[:], offs)
-        nc.sync.dma_start(out=wb[:].bitcast(I32), in_=wb_words[0].bitcast(I32))
         nc.sync.dma_start(out=xw[:].bitcast(I32), in_=xt_words[0].bitcast(I32))
-        load_scale_rows(nc.sync, xs, xt_scales)
         nc.sync.dma_start(ent[:], offs2)
-        nc.sync.dma_start(out=wa[:].bitcast(I32), in_=wa_words[0].rearrange("p n t -> p (n t)").bitcast(I32))
+        load_scale_rows(nc.sync, xs, xt_scales)
         nc.sync.dma_start(out=tbt[0], in_=tb_rows[:, 0, :])
+        nc.sync.dma_start(out=wa[:].bitcast(I32), in_=wa_words[0].rearrange("p n t -> p (n t)").bitcast(I32))
         load_scale_rows(nc.sync, was, wa_scales)
         for t in range(1, PACK - 1):
             nc.sync.dma_start(out=tbt[t], in_=tb_rows[:, t, :])
+        nc.sync.dma_start(out=wb[:].bitcast(I32), in_=wb_words[0].bitcast(I32))
         load_scale_rows(nc.sync, wbs, wb_scales)
         nc.sync.dma_start(out=tbt[PACK - 1], in_=tb_rows[:, PACK - 1, :])
 
         wbd = sb.tile([P, N], U16, name="wbd", align_bytes=64)
         wbsd = sb.tile([P, N], U8, name="wbsd", align_bytes=64)
 
-        nc.vector.tensor_copy(
-            out=wbd[:].rearrange("p (t m) -> p t m", t=PACK), in_=wb[:].rearrange("p (m t) -> p t m", t=PACK)
-        )
         xg = sb.tile([P, J], U16, name="xg", align_bytes=64)
         xsg = sb.tile([P, J], U8, name="xsg", align_bytes=64)
         nc.vector.tensor_copy(out=xg[:], in_=xw[:].indirect(tok[:]))
-        g = sb.tile([P, PACK, J], F32, name="g", align_bytes=64)
+        g_tile = sb.tile([P, PACK * J], F32, name="g_tile", align_bytes=64)
+        g = g_tile[:].rearrange("p (t j) -> p t j", t=PACK)
         nc.vector.tensor_copy(out=xsg[:], in_=xs[:].indirect(tok[:]))
-        for t in range(PACK):
-            nc.vector.tensor_copy(out=g[:, t, :], in_=tbt[t].indirect(ent[:]))
+        for t in range(PACK - 1):
+            nc.vector.tensor_copy(out=g_tile[:, t * J : (t + 1) * J], in_=tbt[t].indirect(ent[:]))
 
         relu_t = []
         for c in range(CHUNKS):
@@ -96,7 +94,7 @@ def tile_list_hidden_plus_table_pl_kernel(
             relu_t.append(ra)
         relu_ps = []
         for c in range(CHUNKS):
-            rp = ps.tile([P, PACK, CH], F32, name="rp%d" % c)
+            rp = ps.tile([P, PACK, CH], F32, name="rp%d" % c, tag="rp%d" % c)
             for t in range(PACK):
                 nc.tensor.transpose(rp[:, t, :], relu_t[c][:, t, :], ident[:])
             relu_ps.append(rp)
@@ -107,14 +105,21 @@ def tile_list_hidden_plus_table_pl_kernel(
         ys = sb.tile([P, J], U8, name="ys", align_bytes=64)
         out_rows = out_0.rearrange("(p t) j -> p t j", t=PACK)
         out_words = out_1[0].rearrange("p j t -> p (j t)").bitcast(I32)
-        hb = [sb.tile([P, CH * PACK], BF16, name="hb%d" % c, align_bytes=64) for c in range(CHUNKS)]
+        hb = [g_tile[:, PACK * J - J // 2 :].bitcast(BF16)]
         yb = [sb.tile([P, CH * PACK], BF16, name="yb%d" % c, align_bytes=64) for c in range(CHUNKS)]
         yf = [sb.tile([P, PACK, CH], F32, name="yf%d" % c, align_bytes=64) for c in range(CHUNKS)]
+
+        def gather_last(h):
+            first = (PACK - 1) * J + h * J // 2
+            nc.vector.tensor_copy(
+                out=g_tile[:, first : first + J // 2],
+                in_=tbt[PACK - 1].indirect(ent[:, h * J // 32 : (h + 1) * J // 32]),
+            )
 
         def add_table(c):
             cols = slice(c * CH, (c + 1) * CH)
             nc.vector.tensor_tensor(
-                out=hb[c][:].rearrange("p (c i t) -> p c t i", i=2, t=PACK),
+                out=hb[c].rearrange("p (c i t) -> p c t i", i=2, t=PACK),
                 in0=relu_ps[c][:].rearrange("p t (c i) -> p c t i", i=2),
                 in1=g[:, :, cols].rearrange("p t (c i) -> p c t i", i=2),
                 op=ADD,
@@ -122,19 +127,21 @@ def tile_list_hidden_plus_table_pl_kernel(
 
         def second_product(c):
             cols = slice(c * CH, (c + 1) * CH)
-            nc.vector.quantize_mx(out=hq[:, cols].bitcast(FP8X4), scales=hs[:, cols], in_=hb[c][:])
-            y = ps.tile([P, PACK, CH], F32, name="y%d" % c, tag="mm%d" % c)
-            for t in range(PACK):
-                w_cols = slice(t * P, (t + 1) * P)
-                nc.tensor.matmul_mx(
-                    out=y[:, t, :], lhsT=wbd[:, w_cols].bitcast(FP4X4), lhsT_scale=wbsd[:, w_cols],
-                    rhs=hq[:, cols].bitcast(FP8X4), rhs_scale=hs[:, cols], start=True, stop=True,
-                )
-            nc.scalar.copy(out=yf[c][:], in_=y[:])
+            nc.vector.quantize_mx(out=hq[:, cols].bitcast(FP8X4), scales=hs[:, cols], in_=hb[c])
+            for u in range(2):
+                y = ps.tile([P, 2, CH], F32, name="y%d_%d" % (c, u), tag=("mm%d", "rp%d")[u] % c)
+                for e in range(2):
+                    w_cols = slice((2 * u + e) * P, (2 * u + e + 1) * P)
+                    nc.tensor.matmul_mx(
+                        out=y[:, e, :], lhsT=wbd[:, w_cols].bitcast(FP4X4), lhsT_scale=wbsd[:, w_cols],
+                        rhs=hq[:, cols].bitcast(FP8X4), rhs_scale=hs[:, cols], start=True, stop=True,
+                    )
+                nc.scalar.copy(out=yf[c][:, 2 * u : 2 * u + 2, :], in_=y[:])
             nc.sync.dma_start(out=out_rows[:, :, cols], in_=yf[c][:])
 
         def round_stored(c):
-            nc.vector.tensor_copy(
+            copy = nc.scalar.copy if c == 0 else nc.vector.tensor_copy
+            copy(
                 out=yb[c][:].rearrange("p (c i t) -> p c t i", i=2, t=PACK),
                 in_=yf[c][:].rearrange("p t (c i) -> p c t i", i=2),
             )
@@ -143,18 +150,31 @@ def tile_list_hidden_plus_table_pl_kernel(
             cols = slice(c * CH, (c + 1) * CH)
             nc.vector.quantize_mx(out=yq[:, cols].bitcast(FP8X4), scales=ys[:, cols], in_=yb[c][:])
 
+        gather_last(0)
+        nc.vector.tensor_copy(
+            out=wbd[:].rearrange("p (t m) -> p t m", t=PACK), in_=wb[:].rearrange("p (m t) -> p t m", t=PACK)
+        )
+        add_table(0)
         nc.vector.tensor_copy(
             out=wbsd[:].rearrange("p (t m) -> p t m", t=PACK), in_=wbs[:].rearrange("p (m t) -> p t m", t=PACK)
         )
-        add_table(0)
         for c in range(1, CHUNKS):
-            add_table(c)
-            second_product(c - 1)
-        second_product(CHUNKS - 1)
+            hb.append(sb.tile([P, CH * PACK], BF16, name="hb%d" % c, align_bytes=64)[:])
+        second_product(0)
         round_stored(0)
-        for c in range(1, CHUNKS):
-            round_stored(c)
-            planes(c - 1)
+        add_table(1)
+        gather_last(1)
+        second_product(1)
+        add_table(2)
+        planes(0)
+        second_product(2)
+        add_table(3)
+        round_stored(1)
+        second_product(3)
+        round_stored(2)
+        planes(1)
+        planes(2)
+        round_stored(3)
         early = slice(0, J - CH)
         nc.sync.dma_start(out=out_words[:, early], in_=yq[:, early].bitcast(I32))
         planes(3)

@@ -14,22 +14,33 @@ U16 = mybir.dt.uint16
 U8 = mybir.dt.uint8
 FP8X4 = mybir.dt.float8_e4m3fn_x4
 FP4X4 = mybir.dt.float4_e2m1fn_x4
-ADD = mybir.AluOpType.add
-RELU = mybir.ActivationFunctionType.Relu
 
 P = 128
 PACK = 4
-QUADS = 4
+QUAD = 32
+SCALE_ROWS = 4
+STRIPE = 16
 CH = 128
 CHUNKS = J // CH
+LAST = PACK - 1
+INNER, OUTER = (1, 2), (0, 3)
 
 
-def load_scale_rows(queue, plane, rows):
-    for q in range(QUADS):
-        queue.dma_start(
-            out=plane[q:P:32, :].bitcast(I32),
-            in_=rows[0, q:16:4, :].bitcast(I32),
-        )
+def load_scale_rows(nc, plane, rows):
+    for i in range(SCALE_ROWS):
+        nc.sync.dma_start(out=plane[i:P:QUAD, :].bitcast(I32), in_=rows[0, i : K // QUAD : SCALE_ROWS, :].bitcast(I32))
+
+
+def as_planes(packed):
+    return packed.rearrange("p (m t) -> p t m", t=PACK)
+
+
+def interleaved(flat):
+    return flat.rearrange("p (c i t) -> p c t i", i=2, t=PACK)
+
+
+def in_pairs(planes):
+    return planes.rearrange("p t (c i) -> p c t i", i=2)
 
 
 def tile_list_hidden_plus_table_pl_kernel(
@@ -40,148 +51,148 @@ def tile_list_hidden_plus_table_pl_kernel(
         sb = ctx.enter_context(tc.tile_pool(name="sb", bufs=1))
         ps = ctx.enter_context(tc.psum_pool(name="ps", bufs=1))
 
-        tok = sb.tile([P, J // 16], U16, name="tok")
-        ent = sb.tile([P, J // 16], U16, name="ent")
-        xw = sb.tile([P, T], U16, name="xw", align_bytes=64)
-        xs = sb.tile([P, T], U8, name="xs", align_bytes=64)
-        wa = sb.tile([P, R], U32, name="wa", align_bytes=64)
-        was = sb.tile([P, R], U8, name="was", align_bytes=64)
-        wb = sb.tile([P, N], U16, name="wb", align_bytes=64)
-        wbs = sb.tile([P, N], U8, name="wbs", align_bytes=64)
-        tbt = [sb.tile([P, V], F32, name="tb%d" % t, align_bytes=64)[:] for t in range(PACK)]
+        tokens = sb.tile([P, J // STRIPE], U16, name="tokens")
+        entries = sb.tile([P, J // STRIPE], U16, name="entries")
+        xt_w = sb.tile([P, T], U16, name="xt_w", align_bytes=64)
+        xt_s = sb.tile([P, T], U8, name="xt_s", align_bytes=64)
+        wa_w = sb.tile([P, R], U32, name="wa_w", align_bytes=64)
+        wa_s = sb.tile([P, R], U8, name="wa_s", align_bytes=64)
+        wb_w = sb.tile([P, N], U16, name="wb_w", align_bytes=64)
+        wb_s = sb.tile([P, N], U8, name="wb_s", align_bytes=64)
+        table = [sb.tile([P, V], F32, name="table%d" % t, align_bytes=64) for t in range(PACK)]
         ident = sb.tile([P, P], F32, name="ident", align_bytes=64)
 
-        nc.vector.memset(xs[:].bitcast(I32), 0)
-        nc.gpsimd.memset(wbs[:].bitcast(I32), 0)
+        nc.vector.memset(xt_s[:].bitcast(I32), 0)
+        nc.gpsimd.memset(wb_s[:].bitcast(I32), 0)
         make_identity(nc, ident[:])
 
-        tb_rows = tb.rearrange("(p t) v -> p t v", t=PACK)
-        nc.sync.dma_start(tok[:], offs)
-        nc.sync.dma_start(out=xw[:].bitcast(I32), in_=xt_words[0].bitcast(I32))
-        nc.sync.dma_start(ent[:], offs2)
-        load_scale_rows(nc.sync, xs, xt_scales)
-        nc.sync.dma_start(out=tbt[0], in_=tb_rows[:, 0, :])
-        nc.sync.dma_start(out=wa[:].bitcast(I32), in_=wa_words[0].rearrange("p n t -> p (n t)").bitcast(I32))
-        load_scale_rows(nc.sync, was, wa_scales)
-        for t in range(1, PACK - 1):
-            nc.sync.dma_start(out=tbt[t], in_=tb_rows[:, t, :])
-        nc.sync.dma_start(out=wb[:].bitcast(I32), in_=wb_words[0].bitcast(I32))
-        load_scale_rows(nc.sync, wbs, wb_scales)
-        nc.sync.dma_start(out=tbt[PACK - 1], in_=tb_rows[:, PACK - 1, :])
+        tb_planes = tb.rearrange("(p t) v -> p t v", t=PACK)
+        nc.sync.dma_start(tokens[:], offs)
+        nc.sync.dma_start(out=xt_w[:].bitcast(I32), in_=xt_words[0].bitcast(I32))
+        nc.sync.dma_start(entries[:], offs2)
+        load_scale_rows(nc, xt_s, xt_scales)
+        nc.sync.dma_start(out=table[0][:], in_=tb_planes[:, 0, :])
+        nc.sync.dma_start(out=wa_w[:].bitcast(I32), in_=wa_words[0].rearrange("p r t -> p (r t)").bitcast(I32))
+        load_scale_rows(nc, wa_s, wa_scales)
+        for t in range(1, LAST):
+            nc.sync.dma_start(out=table[t][:], in_=tb_planes[:, t, :])
+        nc.sync.dma_start(out=wb_w[:].bitcast(I32), in_=wb_words[0].bitcast(I32))
+        load_scale_rows(nc, wb_s, wb_scales)
+        nc.sync.dma_start(out=table[LAST][:], in_=tb_planes[:, LAST, :])
 
-        wbd = sb.tile([P, N], U16, name="wbd", align_bytes=64)
-        wbsd = sb.tile([P, N], U8, name="wbsd", align_bytes=64)
+        x_w = sb.tile([P, J], U16, name="x_w", align_bytes=64)
+        x_s = sb.tile([P, J], U8, name="x_s", align_bytes=64)
+        nc.vector.tensor_copy(out=x_w[:], in_=xt_w[:].indirect(tokens[:]))
+        nc.vector.tensor_copy(out=x_s[:], in_=xt_s[:].indirect(tokens[:]))
 
-        xg = sb.tile([P, J], U16, name="xg", align_bytes=64)
-        xsg = sb.tile([P, J], U8, name="xsg", align_bytes=64)
-        nc.vector.tensor_copy(out=xg[:], in_=xw[:].indirect(tok[:]))
-        g_tile = sb.tile([P, PACK * J], F32, name="g_tile", align_bytes=64)
+        pitch = J + CH
+        g_tile = sb.tile([P, PACK * pitch], F32, name="g_tile", align_bytes=64)
         g = g_tile[:].rearrange("p (t j) -> p t j", t=PACK)
-        nc.vector.tensor_copy(out=xsg[:], in_=xs[:].indirect(tok[:]))
-        for t in range(PACK - 1):
-            nc.vector.tensor_copy(out=g_tile[:, t * J : (t + 1) * J], in_=tbt[t].indirect(ent[:]))
+        for t in range(LAST):
+            nc.vector.tensor_copy(out=g_tile[:, t * pitch : t * pitch + J], in_=table[t][:].indirect(entries[:]))
 
-        relu_t = []
-        for c in range(CHUNKS):
+        relu_rows = {}
+        for c in INNER + OUTER:
             cols = slice(c * CH, (c + 1) * CH)
-            a_t = ps.tile([P, R], F32, name="a_t%d" % c, tag="mm%d" % c)
+            a_rows = ps.tile([P, R], F32, name="a_rows%d" % c, tag="product%d" % c)
             nc.tensor.matmul_mx(
-                out=a_t[:], lhsT=xg[:, cols].bitcast(FP4X4), lhsT_scale=xsg[:, cols],
-                rhs=wa[:].bitcast(FP8X4), rhs_scale=was[:], start=True, stop=True,
+                out=a_rows[:], lhsT=x_w[:, cols].bitcast(FP4X4), lhsT_scale=x_s[:, cols],
+                rhs=wa_w[:].bitcast(FP8X4), rhs_scale=wa_s[:], start=True, stop=True,
             )
-            ra = sb.tile([P, PACK, P], F32, name="ra%d" % c, align_bytes=64)
-            nc.scalar.activation(out=ra[:], in_=a_t[:].rearrange("j (m t) -> j t m", t=PACK), func=RELU)
-            relu_t.append(ra)
-        relu_ps = []
-        for c in range(CHUNKS):
-            rp = ps.tile([P, PACK, CH], F32, name="rp%d" % c, tag="rp%d" % c)
+            relu_rows[c] = sb.tile([P, PACK, P], F32, name="relu_rows%d" % c, align_bytes=64)
+            nc.scalar.activation(
+                out=relu_rows[c][:], in_=as_planes(a_rows[:]), func=mybir.ActivationFunctionType.Relu
+            )
+        relu = {}
+        for c in INNER + OUTER:
+            relu[c] = ps.tile([P, PACK, CH], F32, name="relu%d" % c, tag="turned%d" % c)
             for t in range(PACK):
-                nc.tensor.transpose(rp[:, t, :], relu_t[c][:, t, :], ident[:])
-            relu_ps.append(rp)
+                nc.tensor.transpose(relu[c][:, t, :], relu_rows[c][:, t, :], ident[:])
 
-        hq = sb.tile([P, J], U32, name="hq", align_bytes=64)
-        hs = sb.tile([P, J], U8, name="hs", align_bytes=64)
-        yq = sb.tile([P, J], U32, name="yq", align_bytes=64)
-        ys = sb.tile([P, J], U8, name="ys", align_bytes=64)
-        out_rows = out_0.rearrange("(p t) j -> p t j", t=PACK)
+        last_first = LAST * pitch
+        hid = {
+            INNER[0]: g_tile[:, last_first - CH : last_first + CH].bitcast(BF16),
+            INNER[1]: g_tile[:, last_first + J - CH : last_first + J + CH].bitcast(BF16),
+        }
+        for c in OUTER:
+            hid[c] = sb.tile([P, CH * PACK], BF16, name="hid%d" % c, align_bytes=64)[:]
+        hid_w = sb.tile([P, J], U32, name="hid_w", align_bytes=64)
+        hid_s = sb.tile([P, J], U8, name="hid_s", align_bytes=64)
+        wb_dealt_w = sb.tile([P, N], U16, name="wb_dealt_w", align_bytes=64)
+        wb_dealt_s = sb.tile([P, N], U8, name="wb_dealt_s", align_bytes=64)
+        y = [sb.tile([P, PACK, CH], F32, name="y%d" % c, align_bytes=64) for c in range(CHUNKS)]
+        y_bf = [sb.tile([P, CH * PACK], BF16, name="y_bf%d" % c, align_bytes=64) for c in range(CHUNKS)]
+        y_w = sb.tile([P, J], U32, name="y_w", align_bytes=64)
+        y_s = sb.tile([P, J], U8, name="y_s", align_bytes=64)
+        out_planes = out_0.rearrange("(p t) j -> p t j", t=PACK)
         out_words = out_1[0].rearrange("p j t -> p (j t)").bitcast(I32)
-        hb = [g_tile[:, PACK * J - J // 2 :].bitcast(BF16)]
-        yb = [sb.tile([P, CH * PACK], BF16, name="yb%d" % c, align_bytes=64) for c in range(CHUNKS)]
-        yf = [sb.tile([P, PACK, CH], F32, name="yf%d" % c, align_bytes=64) for c in range(CHUNKS)]
 
-        def gather_last(h):
-            first = (PACK - 1) * J + h * J // 2
-            nc.vector.tensor_copy(
-                out=g_tile[:, first : first + J // 2],
-                in_=tbt[PACK - 1].indirect(ent[:, h * J // 32 : (h + 1) * J // 32]),
-            )
+        def gather_last_plane(c):
+            start = last_first + c * CH
+            offsets = entries[:, c * CH // STRIPE : (c + 1) * CH // STRIPE]
+            nc.vector.tensor_copy(out=g_tile[:, start : start + CH], in_=table[LAST][:].indirect(offsets))
 
         def add_table(c):
-            cols = slice(c * CH, (c + 1) * CH)
             nc.vector.tensor_tensor(
-                out=hb[c].rearrange("p (c i t) -> p c t i", i=2, t=PACK),
-                in0=relu_ps[c][:].rearrange("p t (c i) -> p c t i", i=2),
-                in1=g[:, :, cols].rearrange("p t (c i) -> p c t i", i=2),
-                op=ADD,
+                out=interleaved(hid[c]),
+                in0=in_pairs(relu[c][:]),
+                in1=in_pairs(g[:, :, c * CH : (c + 1) * CH]),
+                op=mybir.AluOpType.add,
             )
 
         def second_product(c):
             cols = slice(c * CH, (c + 1) * CH)
-            nc.vector.quantize_mx(out=hq[:, cols].bitcast(FP8X4), scales=hs[:, cols], in_=hb[c])
-            for u in range(2):
-                y = ps.tile([P, 2, CH], F32, name="y%d_%d" % (c, u), tag=("mm%d", "rp%d")[u] % c)
+            nc.vector.quantize_mx(out=hid_w[:, cols].bitcast(FP8X4), scales=hid_s[:, cols], in_=hid[c])
+            for half, tag in enumerate(("product%d" % c, "turned%d" % c)):
+                bank = ps.tile([P, 2, CH], F32, name="y_bank%d_%d" % (c, half), tag=tag)
                 for e in range(2):
-                    w_cols = slice((2 * u + e) * P, (2 * u + e + 1) * P)
+                    w_cols = slice((2 * half + e) * P, (2 * half + e + 1) * P)
                     nc.tensor.matmul_mx(
-                        out=y[:, e, :], lhsT=wbd[:, w_cols].bitcast(FP4X4), lhsT_scale=wbsd[:, w_cols],
-                        rhs=hq[:, cols].bitcast(FP8X4), rhs_scale=hs[:, cols], start=True, stop=True,
+                        out=bank[:, e, :],
+                        lhsT=wb_dealt_w[:, w_cols].bitcast(FP4X4), lhsT_scale=wb_dealt_s[:, w_cols],
+                        rhs=hid_w[:, cols].bitcast(FP8X4), rhs_scale=hid_s[:, cols], start=True, stop=True,
                     )
-                nc.scalar.copy(out=yf[c][:, 2 * u : 2 * u + 2, :], in_=y[:])
-            nc.sync.dma_start(out=out_rows[:, :, cols], in_=yf[c][:])
+                nc.scalar.copy(out=y[c][:, 2 * half : 2 * half + 2, :], in_=bank[:])
+            nc.sync.dma_start(out=out_planes[:, :, cols], in_=y[c][:])
 
-        def round_stored(c):
-            copy = nc.scalar.copy if c == 0 else nc.vector.tensor_copy
-            copy(
-                out=yb[c][:].rearrange("p (c i t) -> p c t i", i=2, t=PACK),
-                in_=yf[c][:].rearrange("p t (c i) -> p c t i", i=2),
-            )
+        def round_y(c, copy):
+            copy(out=interleaved(y_bf[c][:]), in_=in_pairs(y[c][:]))
 
-        def planes(c):
+        def quantise_y(c):
             cols = slice(c * CH, (c + 1) * CH)
-            nc.vector.quantize_mx(out=yq[:, cols].bitcast(FP8X4), scales=ys[:, cols], in_=yb[c][:])
+            nc.vector.quantize_mx(out=y_w[:, cols].bitcast(FP8X4), scales=y_s[:, cols], in_=y_bf[c][:])
 
-        gather_last(0)
-        nc.vector.tensor_copy(
-            out=wbd[:].rearrange("p (t m) -> p t m", t=PACK), in_=wb[:].rearrange("p (m t) -> p t m", t=PACK)
-        )
-        add_table(0)
-        nc.vector.tensor_copy(
-            out=wbsd[:].rearrange("p (t m) -> p t m", t=PACK), in_=wbs[:].rearrange("p (m t) -> p t m", t=PACK)
-        )
-        for c in range(1, CHUNKS):
-            hb.append(sb.tile([P, CH * PACK], BF16, name="hb%d" % c, align_bytes=64)[:])
-        second_product(0)
-        round_stored(0)
-        add_table(1)
-        gather_last(1)
-        second_product(1)
-        add_table(2)
-        planes(0)
-        second_product(2)
-        add_table(3)
-        round_stored(1)
-        second_product(3)
-        round_stored(2)
-        planes(1)
-        planes(2)
-        round_stored(3)
-        early = slice(0, J - CH)
-        nc.sync.dma_start(out=out_words[:, early], in_=yq[:, early].bitcast(I32))
-        planes(3)
-        late = slice(J - CH, J)
-        nc.sync.dma_start(out=out_words[:, late], in_=yq[:, late].bitcast(I32))
-        for q in range(QUADS):
+        for dealt, packed in ((wb_dealt_w, wb_w), (wb_dealt_s, wb_s)):
+            nc.vector.tensor_copy(out=dealt[:].rearrange("p (t m) -> p t m", t=PACK), in_=as_planes(packed[:]))
+
+        first, second = INNER
+        third, fourth = OUTER
+        gather_last_plane(first)
+        gather_last_plane(second)
+        add_table(first)
+        add_table(second)
+        second_product(first)
+        round_y(first, nc.scalar.copy)
+        gather_last_plane(third)
+        second_product(second)
+        add_table(third)
+        gather_last_plane(fourth)
+        second_product(third)
+        add_table(fourth)
+        quantise_y(first)
+        second_product(fourth)
+        for c in (second, third):
+            round_y(c, nc.vector.tensor_copy)
+            quantise_y(c)
+        early, late = slice(0, fourth * CH), slice(fourth * CH, J)
+        nc.sync.dma_start(out=out_words[:, early], in_=y_w[:, early].bitcast(I32))
+        round_y(fourth, nc.vector.tensor_copy)
+        quantise_y(fourth)
+        nc.sync.dma_start(out=out_words[:, late], in_=y_w[:, late].bitcast(I32))
+
+        for q in range(P // QUAD):
             queue = nc.sync if q % 2 == 0 else nc.scalar
             queue.dma_start(
-                out=out_2[0, 4 * q : 4 * q + 4, :].bitcast(I32), in_=ys[32 * q : 32 * q + 4, :].bitcast(I32)
+                out=out_2[0, SCALE_ROWS * q : SCALE_ROWS * (q + 1), :].bitcast(I32),
+                in_=y_s[QUAD * q : QUAD * q + SCALE_ROWS, :].bitcast(I32),
             )

from contextlib import ExitStack

import concourse.mybir as mybir
from concourse.masks import make_identity

K, T, J, R, V, N = 512, 2048, 512, 512, 1024, 512
FLOPS = 2 * K * R * J + 2 * R * N * J

F32 = mybir.dt.float32
BF16 = mybir.dt.bfloat16
I32 = mybir.dt.int32
U32 = mybir.dt.uint32
U16 = mybir.dt.uint16
U8 = mybir.dt.uint8
FP8X4 = mybir.dt.float8_e4m3fn_x4
FP4X4 = mybir.dt.float4_e2m1fn_x4

P = 128
PACK = 4
QUAD = 32
SCALE_ROWS = 4
STRIPE = 16
CH = 128
CHUNKS = J // CH
LAST = PACK - 1
INNER, OUTER = (1, 2), (0, 3)


def load_scale_rows(nc, plane, rows):
    for i in range(SCALE_ROWS):
        nc.sync.dma_start(out=plane[i:P:QUAD, :].bitcast(I32), in_=rows[0, i : K // QUAD : SCALE_ROWS, :].bitcast(I32))


def as_planes(packed):
    return packed.rearrange("p (m t) -> p t m", t=PACK)


def interleaved(flat):
    return flat.rearrange("p (c i t) -> p c t i", i=2, t=PACK)


def in_pairs(planes):
    return planes.rearrange("p t (c i) -> p c t i", i=2)


def tile_list_hidden_plus_table_pl_kernel(
    tc, xt_words, xt_scales, wa_words, wa_scales, tb, wb_words, wb_scales, offs, offs2, out_0, out_1, out_2
):
    nc = tc.nc
    with ExitStack() as ctx:
        sb = ctx.enter_context(tc.tile_pool(name="sb", bufs=1))
        ps = ctx.enter_context(tc.psum_pool(name="ps", bufs=1))

        tokens = sb.tile([P, J // STRIPE], U16, name="tokens")
        entries = sb.tile([P, J // STRIPE], U16, name="entries")
        xt_w = sb.tile([P, T], U16, name="xt_w", align_bytes=64)
        xt_s = sb.tile([P, T], U8, name="xt_s", align_bytes=64)
        wa_w = sb.tile([P, R], U32, name="wa_w", align_bytes=64)
        wa_s = sb.tile([P, R], U8, name="wa_s", align_bytes=64)
        wb_w = sb.tile([P, N], U16, name="wb_w", align_bytes=64)
        wb_s = sb.tile([P, N], U8, name="wb_s", align_bytes=64)
        table = [sb.tile([P, V], F32, name="table%d" % t, align_bytes=64) for t in range(PACK)]
        ident = sb.tile([P, P], F32, name="ident", align_bytes=64)

        nc.vector.memset(xt_s[:].bitcast(I32), 0)
        nc.gpsimd.memset(wb_s[:].bitcast(I32), 0)
        make_identity(nc, ident[:])

        tb_planes = tb.rearrange("(p t) v -> p t v", t=PACK)
        nc.sync.dma_start(tokens[:], offs)
        nc.sync.dma_start(out=xt_w[:].bitcast(I32), in_=xt_words[0].bitcast(I32))
        nc.sync.dma_start(entries[:], offs2)
        load_scale_rows(nc, xt_s, xt_scales)
        nc.sync.dma_start(out=table[0][:], in_=tb_planes[:, 0, :])
        nc.sync.dma_start(out=wa_w[:].bitcast(I32), in_=wa_words[0].rearrange("p r t -> p (r t)").bitcast(I32))
        load_scale_rows(nc, wa_s, wa_scales)
        for t in range(1, LAST):
            nc.sync.dma_start(out=table[t][:], in_=tb_planes[:, t, :])
        nc.sync.dma_start(out=wb_w[:].bitcast(I32), in_=wb_words[0].bitcast(I32))
        load_scale_rows(nc, wb_s, wb_scales)
        nc.sync.dma_start(out=table[LAST][:], in_=tb_planes[:, LAST, :])

        x_w = sb.tile([P, J], U16, name="x_w", align_bytes=64)
        x_s = sb.tile([P, J], U8, name="x_s", align_bytes=64)
        nc.vector.tensor_copy(out=x_w[:], in_=xt_w[:].indirect(tokens[:]))
        nc.vector.tensor_copy(out=x_s[:], in_=xt_s[:].indirect(tokens[:]))

        pitch = J + CH
        g_tile = sb.tile([P, PACK * pitch], F32, name="g_tile", align_bytes=64)
        g = g_tile[:].rearrange("p (t j) -> p t j", t=PACK)
        for t in range(LAST):
            nc.vector.tensor_copy(out=g_tile[:, t * pitch : t * pitch + J], in_=table[t][:].indirect(entries[:]))

        relu_rows = {}
        for c in INNER + OUTER:
            cols = slice(c * CH, (c + 1) * CH)
            a_rows = ps.tile([P, R], F32, name="a_rows%d" % c, tag="product%d" % c)
            nc.tensor.matmul_mx(
                out=a_rows[:], lhsT=x_w[:, cols].bitcast(FP4X4), lhsT_scale=x_s[:, cols],
                rhs=wa_w[:].bitcast(FP8X4), rhs_scale=wa_s[:], start=True, stop=True,
            )
            relu_rows[c] = sb.tile([P, PACK, P], F32, name="relu_rows%d" % c, align_bytes=64)
            nc.scalar.activation(
                out=relu_rows[c][:], in_=as_planes(a_rows[:]), func=mybir.ActivationFunctionType.Relu
            )
        relu = {}
        for c in INNER + OUTER:
            relu[c] = ps.tile([P, PACK, CH], F32, name="relu%d" % c, tag="turned%d" % c)
            for t in range(PACK):
                nc.tensor.transpose(relu[c][:, t, :], relu_rows[c][:, t, :], ident[:])

        last_first = LAST * pitch
        hid = {
            INNER[0]: g_tile[:, last_first - CH : last_first + CH].bitcast(BF16),
            INNER[1]: g_tile[:, last_first + J - CH : last_first + J + CH].bitcast(BF16),
        }
        for c in OUTER:
            hid[c] = sb.tile([P, CH * PACK], BF16, name="hid%d" % c, align_bytes=64)[:]
        hid_w = sb.tile([P, J], U32, name="hid_w", align_bytes=64)
        hid_s = sb.tile([P, J], U8, name="hid_s", align_bytes=64)
        wb_dealt_w = sb.tile([P, N], U16, name="wb_dealt_w", align_bytes=64)
        wb_dealt_s = sb.tile([P, N], U8, name="wb_dealt_s", align_bytes=64)
        y = [sb.tile([P, PACK, CH], F32, name="y%d" % c, align_bytes=64) for c in range(CHUNKS)]
        y_bf = [sb.tile([P, CH * PACK], BF16, name="y_bf%d" % c, align_bytes=64) for c in range(CHUNKS)]
        y_w = sb.tile([P, J], U32, name="y_w", align_bytes=64)
        y_s = sb.tile([P, J], U8, name="y_s", align_bytes=64)
        out_planes = out_0.rearrange("(p t) j -> p t j", t=PACK)
        out_words = out_1[0].rearrange("p j t -> p (j t)").bitcast(I32)

        def gather_last_plane(c):
            start = last_first + c * CH
            offsets = entries[:, c * CH // STRIPE : (c + 1) * CH // STRIPE]
            nc.vector.tensor_copy(out=g_tile[:, start : start + CH], in_=table[LAST][:].indirect(offsets))

        def add_table(c):
            nc.vector.tensor_tensor(
                out=interleaved(hid[c]),
                in0=in_pairs(relu[c][:]),
                in1=in_pairs(g[:, :, c * CH : (c + 1) * CH]),
                op=mybir.AluOpType.add,
            )

        def second_product(c):
            cols = slice(c * CH, (c + 1) * CH)
            nc.vector.quantize_mx(out=hid_w[:, cols].bitcast(FP8X4), scales=hid_s[:, cols], in_=hid[c])
            for half, tag in enumerate(("product%d" % c, "turned%d" % c)):
                bank = ps.tile([P, 2, CH], F32, name="y_bank%d_%d" % (c, half), tag=tag)
                for e in range(2):
                    w_cols = slice((2 * half + e) * P, (2 * half + e + 1) * P)
                    nc.tensor.matmul_mx(
                        out=bank[:, e, :],
                        lhsT=wb_dealt_w[:, w_cols].bitcast(FP4X4), lhsT_scale=wb_dealt_s[:, w_cols],
                        rhs=hid_w[:, cols].bitcast(FP8X4), rhs_scale=hid_s[:, cols], start=True, stop=True,
                    )
                nc.scalar.copy(out=y[c][:, 2 * half : 2 * half + 2, :], in_=bank[:])
            nc.sync.dma_start(out=out_planes[:, :, cols], in_=y[c][:])

        def round_y(c, copy):
            copy(out=interleaved(y_bf[c][:]), in_=in_pairs(y[c][:]))

        def quantise_y(c):
            cols = slice(c * CH, (c + 1) * CH)
            nc.vector.quantize_mx(out=y_w[:, cols].bitcast(FP8X4), scales=y_s[:, cols], in_=y_bf[c][:])

        for dealt, packed in ((wb_dealt_w, wb_w), (wb_dealt_s, wb_s)):
            nc.vector.tensor_copy(out=dealt[:].rearrange("p (t m) -> p t m", t=PACK), in_=as_planes(packed[:]))

        first, second = INNER
        third, fourth = OUTER
        gather_last_plane(first)
        gather_last_plane(second)
        add_table(first)
        add_table(second)
        second_product(first)
        round_y(first, nc.scalar.copy)
        gather_last_plane(third)
        second_product(second)
        add_table(third)
        gather_last_plane(fourth)
        second_product(third)
        add_table(fourth)
        quantise_y(first)
        second_product(fourth)
        for c in (second, third):
            round_y(c, nc.vector.tensor_copy)
            quantise_y(c)
        early, late = slice(0, fourth * CH), slice(fourth * CH, J)
        nc.sync.dma_start(out=out_words[:, early], in_=y_w[:, early].bitcast(I32))
        round_y(fourth, nc.vector.tensor_copy)
        quantise_y(fourth)
        nc.sync.dma_start(out=out_words[:, late], in_=y_w[:, late].bitcast(I32))

        for q in range(P // QUAD):
            queue = nc.sync if q % 2 == 0 else nc.scalar
            queue.dma_start(
                out=out_2[0, SCALE_ROWS * q : SCALE_ROWS * (q + 1), :].bitcast(I32),
                in_=y_s[QUAD * q : QUAD * q + SCALE_ROWS, :].bitcast(I32),
            )
